import numpy as np
import ml_dtypes


def mxq(x, axis, fmt="e4m3"):
    dtype, down = {"e4m3": (ml_dtypes.float8_e4m3fn, 7), "e5m2": (ml_dtypes.float8_e5m2, 14)}[fmt]
    v = np.moveaxis(np.asarray(x, np.float32).astype(ml_dtypes.bfloat16).astype(np.float64), axis, -1)
    blocks = v.reshape(v.shape[:-1] + (-1, 32))
    amax = np.abs(blocks).max(-1, keepdims=True)
    byte = np.maximum(np.where(amax > 0, np.frexp(amax)[1] - 1 + 127, 0) - down, 1)
    scale = np.exp2(byte - 127.0)
    codes = (blocks / scale).astype(np.float32).astype(dtype).astype(np.float64)
    return np.moveaxis((codes * scale).reshape(v.shape), -1, axis)


WIDE = False


def mx_kscale(k):
    if not WIDE:
        return np.ones(k)
    levels = np.array([10, -10, 5, -5, 0])
    if k % 512:
        return np.exp2(np.random.permutation(np.resize(levels, k // 32))).repeat(32)
    a = np.empty((k // 512, 16))
    for p in range(k // 512):
        a[p, :8] = np.random.permutation(np.resize(levels, 8))
        for g in range(8):
            far = levels[np.abs(levels - a[p, g]) >= 10]
            a[p, g + 8] = far[np.random.randint(len(far))]
    return np.exp2(a.ravel()).repeat(32)


def f64(x):
    return np.asarray(x).astype(np.float64)


E2M1 = np.array([0.0, 0.5, 1.0, 1.5, 2.0, 3.0, 4.0, 6.0, -0.0, -0.5, -1.0, -1.5, -2.0, -3.0, -4.0, -6.0])


def pack_weight(w, fmt):
    k, n = w.shape
    w = f64(np.asarray(w, np.float32).astype(ml_dtypes.bfloat16)).reshape(k // 32, 32, n)
    amax = np.abs(w).max(1)
    if fmt == "e4m3":
        byte = np.frexp(amax)[1] - 1 + 127 - 7
    else:
        mant, ex = np.frexp(amax / 6.0)
        byte = np.where(mant > 0.5, ex, ex - 1) + 127
    byte = np.clip(np.where(amax > 0, byte, 1), 1, 254)
    scaled = (w * np.exp2(127.0 - byte)[:, None, :]).reshape(k, n).astype(np.float32)
    by_word = np.ascontiguousarray(scaled.reshape(k // 512, 128, 4, n).transpose(0, 1, 3, 2))
    if fmt == "e4m3":
        words = by_word.astype(ml_dtypes.float8_e4m3fn).view(np.uint8)
    else:
        c = by_word.astype(ml_dtypes.float4_e2m1fn).view(np.uint8) & 0xF
        words = (c[..., 0::2] | (c[..., 1::2] << 4)).reshape(k // 512, 128, 2 * n)
    return np.ascontiguousarray(words), np.ascontiguousarray(byte.astype(np.uint8).reshape(k // 512, 16, n))


def unpack_weight(words, scales, fmt):
    g, _, n = scales.shape
    words = np.ascontiguousarray(words).reshape(g, 128, n, -1)
    if fmt == "e4m3":
        vals = words.view(ml_dtypes.float8_e4m3fn).astype(np.float64)
    else:
        nib = np.empty((g, 128, n, 4), np.uint8)
        nib[..., 0::2] = words & 0xF
        nib[..., 1::2] = words >> 4
        vals = E2M1[nib]
    vals = vals * np.repeat(np.exp2(scales.astype(np.float64) - 127.0), 8, axis=1)[..., None]
    return vals.transpose(0, 1, 3, 2).reshape(g * 512, n)


def softplus(v):
    return np.log(1.0 + np.exp(v))


K, L, T, N = 1024, 1024, 512, 512


def setup_inputs():
    n = np.random.standard_normal
    fk = mx_kscale(K)
    fl = mx_kscale(L)
    xtp = pack_weight(n((K, T)) / fk[:, None], "e4m3")
    xqp = pack_weight(n((L, T)) / fl[:, None], "e2m1")
    wqp = pack_weight(n((L, N)) * 1 / np.sqrt(L) * fl[:, None], "e4m3")
    vbp = pack_weight(n((K, N)) * 1 / np.sqrt(K) * fk[:, None], "e2m1")
    vap = pack_weight(n((L, N)) * 1 / np.sqrt(L) * fl[:, None], "e4m3")
    return {
        "xt_words": xtp[0],
        "xt_scales": xtp[1],
        "wa": (n((K, N)) * 1 / np.sqrt(K) * fk[:, None]).astype(np.float32),
        "xq_words": xqp[0],
        "xq_scales": xqp[1],
        "wq_words": wqp[0],
        "wq_scales": wqp[1],
        "vb_words": vbp[0],
        "vb_scales": vbp[1],
        "va_words": vap[0],
        "va_scales": vap[1],
    }


def reference(xt_words, xt_scales, wa, xq_words, xq_scales, wq_words, wq_scales, vb_words, vb_scales, va_words, va_scales):
    xtu = unpack_weight(xt_words, xt_scales, "e4m3")
    xqu = unpack_weight(xq_words, xq_scales, "e2m1")
    wqu = unpack_weight(wq_words, wq_scales, "e4m3")
    vbu = unpack_weight(vb_words, vb_scales, "e2m1")
    vau = unpack_weight(va_words, va_scales, "e4m3")
    waq = mxq(f64(wa), 0, "e4m3")
    a = waq.T @ xtu
    b = wqu.T @ xqu
    u = vau.T @ xqu
    v = vbu.T @ xtu
    pa = softplus(u)
    pb = softplus(v)
    y = (pa * a + pb * b) / (pa + pb + 0.1)
    return y

@@ -1,0 +1,200 @@
+from contextlib import ExitStack
+
+import concourse.mybir as mybir
+
+K, T, N = 1024, 512, 512
+FLOPS = 4 * 2 * K * T * N
+
+F32 = mybir.dt.float32
+BF16 = mybir.dt.bfloat16
+I32 = mybir.dt.int32
+U32 = mybir.dt.uint32
+U8 = mybir.dt.uint8
+FP8X4 = mybir.dt.float8_e4m3fn_x4
+FP4X4 = mybir.dt.float4_e2m1fn_x4
+ACT = mybir.ActivationFunctionType
+ALU = mybir.AluOpType
+
+P = 128
+PACK = 4
+PASSES = K // (P * PACK)
+TILES = N // P
+HALF = N // 2
+TINY = 2.0**-46
+
+
+def tile_mix_precision_weighted_sums_kernel(
+    tc, xt_words, xt_scales, wa, xq_words, xq_scales, wq_words, wq_scales, vb_words, vb_scales, va_words, va_scales, out
+):
+    nc = tc.nc
+    with ExitStack() as ctx:
+        keep = ctx.enter_context(tc.tile_pool(name="keep", bufs=1))
+        psum = ctx.enter_context(tc.psum_pool(name="psum", bufs=1))
+        ctx.enter_context(tc.manual_schedule())
+
+        def plane_tile(name):
+            plane = keep.tile([P, PASSES, 512], U8, name=name, align_bytes=64)
+            nc.vector.memset(plane[:].bitcast(I32), 0)
+            return plane
+
+        def load_scales(queue, plane, scales, quadrants):
+            for q in quadrants:
+                queue.dma_start(
+                    out=plane[32 * q : 32 * q + 4, :, :].bitcast(I32),
+                    in_=scales[:, 4 * q : 4 * q + 4, :].rearrange("g r n -> r g n").bitcast(I32),
+                )
+
+        def load_fp8(name, words):
+            codes = keep.tile([P, PASSES, 512], U32, name=name, align_bytes=64)
+            nc.sync.dma_start(out=codes[:].bitcast(I32), in_=words.rearrange("g p n t -> p g (n t)").bitcast(I32))
+            return codes
+
+        def load_fp4(name, words):
+            codes = keep.tile([P, PASSES, 1024], U8, name=name, align_bytes=64)
+            nc.sync.dma_start(out=codes[:].bitcast(I32), in_=words.rearrange("g p b -> p g b").bitcast(I32))
+            return codes
+
+        xq_s = plane_tile("xq_s")
+        va_s = plane_tile("va_s")
+        vb_s = plane_tile("vb_s")
+        xt_s = plane_tile("xt_s")
+        wq_s = plane_tile("wq_s")
+        warm = keep.tile([P, 8], F32, name="warm")
+        nc.vector.memset(warm[:], 0.0)
+
+        warm_out = keep.tile([P, 8], F32, name="warm_out")
+        nc.scalar.activation(out=warm_out[:], in_=warm[:], func=ACT.Sigmoid)
+        xq = load_fp4("xq", xq_words)
+        load_scales(nc.sync, xq_s, xq_scales, range(4))
+        load_scales(nc.sync, va_s, va_scales, range(2))
+        va = load_fp8("va", va_words)
+        load_scales(nc.sync, va_s, va_scales, range(2, 4))
+        load_scales(nc.gpsimd, vb_s, vb_scales, range(2, 4))
+        load_scales(nc.gpsimd, wq_s, wq_scales, range(4))
+        vb = load_fp4("vb", vb_words)
+        xt = load_fp8("xt", xt_words)
+        load_scales(nc.sync, xt_s, xt_scales, range(4))
+        load_scales(nc.sync, vb_s, vb_scales, range(2))
+
+        pieces = [(g, h) for h in range(2) for g in range(PASSES)]
+        wa_raw = {}
+        for g, h in pieces:
+            raw = keep.tile([P, PACK, HALF], F32, name="wa_raw%d%d" % (g, h))
+            nc.sync.dma_start(
+                out=raw[:],
+                in_=wa[512 * g : 512 * (g + 1), HALF * h : HALF * (h + 1)].rearrange("(p j) n -> p j n", j=PACK),
+            )
+            wa_raw[g, h] = raw
+        wq = load_fp8("wq", wq_words)
+
+        def product(bank, lhs, rhs):
+            acc = psum.tile([P, T], F32, name=bank, tag=bank)
+            for g in range(PASSES):
+                lc, ls = lhs(g)
+                rc, rs = rhs(g)
+                nc.tensor.matmul_mx(
+                    out=acc[:], lhsT=lc, lhsT_scale=ls, rhs=rc, rhs_scale=rs, start=(g == 0), stop=(g == PASSES - 1)
+                )
+            return acc
+
+        def xq_pass(g):
+            return xq[:, g, :].bitcast(FP4X4), xq_s[:, g, :]
+
+        def xt_pass(g):
+            return xt[:, g, :].bitcast(FP8X4), xt_s[:, g, :]
+
+        def fp8_cols(codes, plane, i):
+            return lambda g: (codes[:, g, P * i : P * (i + 1)].bitcast(FP8X4), plane[:, g, P * i : P * (i + 1)])
+
+        def fp4_cols(codes, plane, i):
+            return lambda g: (codes[:, g, 2 * P * i : 2 * P * (i + 1)].bitcast(FP4X4), plane[:, g, P * i : P * (i + 1)])
+
+        def work(name):
+            return keep.tile([P, T], F32, name=name)
+
+        u = [product("first%d" % i, fp8_cols(va, va_s, i), xq_pass) for i in range(TILES)]
+        v = [product("second%d" % i, fp4_cols(vb, vb_s, i), xt_pass) for i in range(TILES)]
+
+        su = [work("su%d" % i) for i in range(TILES)]
+        sv = [work("sv%d" % i) for i in range(TILES)]
+        for i in range(TILES):
+            nc.scalar.activation(out=su[i][:], in_=u[i][:], func=ACT.Sigmoid, scale=-1.0)
+        for i in range(TILES):
+            nc.scalar.activation(out=sv[i][:], in_=v[i][:], func=ACT.Sigmoid, scale=-1.0)
+
+        wa_codes, wa_planes, grouped = {}, {}, {}
+
+        def cast(key):
+            wide = keep.tile([P, HALF, PACK], BF16, name="grouped%d%d" % key, align_bytes=64)
+            nc.vector.tensor_copy(
+                out=wide[:].rearrange("p (c i) j -> p c j i", i=4),
+                in_=wa_raw[key][:].rearrange("p j (c i) -> p c j i", i=4),
+            )
+            grouped[key] = wide
+
+        def quantize(key):
+            codes = keep.tile([P, HALF], U32, name="wa_codes%d%d" % key, align_bytes=64)
+            plane = keep.tile([P, HALF], U8, name="wa_plane%d%d" % key, align_bytes=64)
+            nc.vector.quantize_mx(
+                out=codes[:].bitcast(FP8X4), scales=plane[:], in_=grouped[key][:].rearrange("p c j -> p (c j)")
+            )
+            wa_codes[key], wa_planes[key] = codes, plane
+
+        cast(pieces[0])
+        for n in range(1, len(pieces)):
+            cast(pieces[n])
+            quantize(pieces[n - 1])
+
+        def wa_cols(i):
+            h, c = divmod(i, 2)
+            return lambda g: (
+                wa_codes[g, h][:, P * c : P * (c + 1)].bitcast(FP8X4),
+                wa_planes[g, h][:, P * c : P * (c + 1)],
+            )
+
+        def softplus(name, sig, pre):
+            log_sig = work("ln_" + name)
+            nc.scalar.activation(out=log_sig[:], in_=sig[:], func=ACT.Ln, bias=TINY)
+            result = work(name)
+            nc.vector.scalar_tensor_tensor(
+                out=result[:], in0=log_sig[:], scalar=-1.0, in1=pre[:], op0=ALU.mult, op1=ALU.max
+            )
+            return result
+
+        pa, pb, total, a, b = [], [], [], [], []
+        for i in range(TILES):
+            pa.append(softplus("pa%d" % i, su[i], u[i]))
+            if i == 0:
+                quantize(pieces[-1])
+            pb.append(softplus("pb%d" % i, sv[i], v[i]))
+            total.append(work("total%d" % i))
+            nc.gpsimd.tensor_tensor(out=total[i][:], in0=pa[i][:], in1=pb[i][:], op=ALU.add)
+            a.append(product("first%d" % i, wa_cols(i), xt_pass))
+            b.append(product("second%d" % i, fp8_cols(wq, wq_s, i), xq_pass))
+
+        root = [work("root%d" % i) for i in range(TILES)]
+        inverse = [work("inverse%d" % i) for i in range(TILES)]
+        for i in range(TILES):
+            nc.scalar.activation(out=root[i][:], in_=total[i][:], func=ACT.Abs_reciprocal_sqrt, bias=0.1)
+            nc.scalar.activation(out=inverse[i][:], in_=root[i][:], func=ACT.Square)
+
+        na = [work("na%d" % i) for i in range(TILES)]
+        nb = [work("nb%d" % i) for i in range(TILES)]
+        num = [work("num%d" % i) for i in range(TILES)]
+        for i in range(TILES):
+            nc.vector.tensor_tensor(out=na[i][:], in0=a[i][:], in1=pa[i][:], op=ALU.mult)
+            nc.vector.tensor_tensor(out=nb[i][:], in0=b[i][:], in1=pb[i][:], op=ALU.mult)
+            if i < 2:
+                nc.gpsimd.tensor_tensor(out=num[i][:], in0=na[i][:], in1=nb[i][:], op=ALU.add)
+
+        def finish(i):
+            y = work("y%d" % i)
+            nc.vector.tensor_tensor(out=y[:], in0=num[i][:], in1=inverse[i][:], op=ALU.mult)
+            nc.sync.dma_start(out=out[P * i : P * (i + 1), :], in_=y[:])
+
+        finish(0)
+        nc.vector.tensor_tensor(out=num[2][:], in0=na[2][:], in1=nb[2][:], op=ALU.add)
+        finish(1)
+        nc.vector.tensor_tensor(out=num[3][:], in0=na[3][:], in1=nb[3][:], op=ALU.add)
+        finish(2)
+        finish(3)

@@ -21,6 +21,8 @@ PASSES = K // (P * PACK)
 TILES = N // P
 HALF = N // 2
 TINY = 2.0**-46
+WARM_NARROW = 10
+WARM_WIDE = 4
 
 
 def tile_mix_precision_weighted_sums_kernel(
@@ -56,7 +58,12 @@ def tile_mix_precision_weighted_sums_kernel(
 
         xq_s = plane_tile("xq_s")
         va_s = plane_tile("va_s")
+        ones = keep.tile([P, PACK * P], BF16, name="ones", align_bytes=64)
+        nc.vector.memset(ones[:], 1.0)
         vb_s = plane_tile("vb_s")
+        ones_codes = keep.tile([P, P], U32, name="ones_codes", align_bytes=64)
+        ones_plane = keep.tile([P, P], U8, name="ones_plane", align_bytes=64)
+        nc.vector.quantize_mx(out=ones_codes[:].bitcast(FP8X4), scales=ones_plane[:], in_=ones[:])
         xt_s = plane_tile("xt_s")
         wq_s = plane_tile("wq_s")
         warm = keep.tile([P, 8], F32, name="warm")
@@ -76,15 +83,16 @@ def tile_mix_precision_weighted_sums_kernel(
         load_scales(nc.sync, xt_s, xt_scales, range(4))
         load_scales(nc.sync, vb_s, vb_scales, range(2))
 
-        pieces = [(g, h) for h in range(2) for g in range(PASSES)]
-        wa_raw = {}
-        for g, h in pieces:
-            raw = keep.tile([P, PACK, HALF], F32, name="wa_raw%d%d" % (g, h))
-            nc.sync.dma_start(
-                out=raw[:],
-                in_=wa[512 * g : 512 * (g + 1), HALF * h : HALF * (h + 1)].rearrange("(p j) n -> p j n", j=PACK),
-            )
-            wa_raw[g, h] = raw
+        def load_wa(g, cols):
+            raw = keep.tile([P, PACK, cols.stop - cols.start], F32, name="wa_raw%d_%d" % (g, cols.start))
+            nc.sync.dma_start(out=raw[:], in_=wa[512 * g : 512 * (g + 1), cols].rearrange("(p j) n -> p j n", j=PACK))
+            return raw
+
+        pieces = [(g, h) for g in range(PASSES) for h in range(2)]
+        first_pass = load_wa(0, slice(0, N))
+        wa_raw = {(0, h): first_pass[:, :, HALF * h : HALF * (h + 1)] for h in range(2)}
+        for h in range(2):
+            wa_raw[1, h] = load_wa(1, slice(HALF * h, HALF * (h + 1)))[:]
         wq = load_fp8("wq", wq_words)
 
         def product(bank, lhs, rhs):
@@ -112,6 +120,13 @@ def tile_mix_precision_weighted_sums_kernel(
         def work(name):
             return keep.tile([P, T], F32, name=name)
 
+        idle = psum.tile([P, T], F32, name="idle", tag="second3")
+        ones_mx = dict(lhsT=ones_codes[:].bitcast(FP8X4), lhsT_scale=ones_plane[:], start=True, stop=True)
+        for n in range(WARM_NARROW):
+            nc.tensor.matmul_mx(out=idle[:, 0:P], rhs=ones_codes[:].bitcast(FP8X4), rhs_scale=ones_plane[:], **ones_mx)
+        for n in range(WARM_WIDE):
+            nc.tensor.matmul_mx(out=idle[:], rhs=xq_pass(0)[0], rhs_scale=xq_pass(0)[1], **ones_mx)
+
         u = [product("first%d" % i, fp8_cols(va, va_s, i), xq_pass) for i in range(TILES)]
         v = [product("second%d" % i, fp4_cols(vb, vb_s, i), xt_pass) for i in range(TILES)]
 
@@ -128,7 +143,7 @@ def tile_mix_precision_weighted_sums_kernel(
             wide = keep.tile([P, HALF, PACK], BF16, name="grouped%d%d" % key, align_bytes=64)
             nc.vector.tensor_copy(
                 out=wide[:].rearrange("p (c i) j -> p c j i", i=4),
-                in_=wa_raw[key][:].rearrange("p j (c i) -> p c j i", i=4),
+                in_=wa_raw[key].rearrange("p j (c i) -> p c j i", i=4),
             )
             grouped[key] = wide
 
@@ -144,6 +159,7 @@ def tile_mix_precision_weighted_sums_kernel(
         for n in range(1, len(pieces)):
             cast(pieces[n])
             quantize(pieces[n - 1])
+        quantize(pieces[-1])
 
         def wa_cols(i):
             h, c = divmod(i, 2)
@@ -164,8 +180,6 @@ def tile_mix_precision_weighted_sums_kernel(
         pa, pb, total, a, b = [], [], [], [], []
         for i in range(TILES):
             pa.append(softplus("pa%d" % i, su[i], u[i]))
-            if i == 0:
-                quantize(pieces[-1])
             pb.append(softplus("pb%d" % i, sv[i], v[i]))
             total.append(work("total%d" % i))
             nc.gpsimd.tensor_tensor(out=total[i][:], in0=pa[i][:], in1=pb[i][:], op=ALU.add)
@@ -187,14 +201,17 @@ def tile_mix_precision_weighted_sums_kernel(
             if i < 2:
                 nc.gpsimd.tensor_tensor(out=num[i][:], in0=na[i][:], in1=nb[i][:], op=ALU.add)
 
-        def finish(i):
-            y = work("y%d" % i)
-            nc.vector.tensor_tensor(out=y[:], in0=num[i][:], in1=inverse[i][:], op=ALU.mult)
-            nc.sync.dma_start(out=out[P * i : P * (i + 1), :], in_=y[:])
+        def finish(i, parts=1):
+            width = T // parts
+            for c in range(0, T, width):
+                y = keep.tile([P, width], F32, name="y%d_%d" % (i, c))
+                cols = slice(c, c + width)
+                nc.vector.tensor_tensor(out=y[:], in0=num[i][:, cols], in1=inverse[i][:, cols], op=ALU.mult)
+                nc.sync.dma_start(out=out[P * i : P * (i + 1), cols], in_=y[:])
 
         finish(0)
         nc.vector.tensor_tensor(out=num[2][:], in0=na[2][:], in1=nb[2][:], op=ALU.add)
         finish(1)
         nc.vector.tensor_tensor(out=num[3][:], in0=na[3][:], in1=nb[3][:], op=ALU.add)
         finish(2)
-        finish(3)
+        finish(3, 2)

@@ -88,11 +88,8 @@ def tile_mix_precision_weighted_sums_kernel(
             nc.sync.dma_start(out=raw[:], in_=wa[512 * g : 512 * (g + 1), cols].rearrange("(p j) n -> p j n", j=PACK))
             return raw
 
-        pieces = [(g, h) for g in range(PASSES) for h in range(2)]
-        first_pass = load_wa(0, slice(0, N))
-        wa_raw = {(0, h): first_pass[:, :, HALF * h : HALF * (h + 1)] for h in range(2)}
-        for h in range(2):
-            wa_raw[1, h] = load_wa(1, slice(HALF * h, HALF * (h + 1)))[:]
+        pieces = [(0, 0, 256), (0, 256, 512), (1, 0, 256), (1, 256, 384), (1, 384, 512)]
+        wa_raw = [load_wa(g, slice(lo, hi)) for g, lo, hi in pieces]
         wq = load_fp8("wq", wq_words)
 
         def product(bank, lhs, rhs):
@@ -137,36 +134,30 @@ def tile_mix_precision_weighted_sums_kernel(
         for i in range(TILES):
             nc.scalar.activation(out=sv[i][:], in_=v[i][:], func=ACT.Sigmoid, scale=-1.0)
 
-        wa_codes, wa_planes, grouped = {}, {}, {}
+        wa_codes = keep.tile([P, PASSES, N], U32, name="wa_codes", align_bytes=64)
+        wa_s = keep.tile([P, PASSES, N], U8, name="wa_s", align_bytes=64)
 
-        def cast(key):
-            wide = keep.tile([P, HALF, PACK], BF16, name="grouped%d%d" % key, align_bytes=64)
+        def cast(n):
+            g, lo, hi = pieces[n]
+            grouped = keep.tile([P, hi - lo, PACK], BF16, name="grouped%d" % n, align_bytes=64)
             nc.vector.tensor_copy(
-                out=wide[:].rearrange("p (c i) j -> p c j i", i=4),
-                in_=wa_raw[key].rearrange("p j (c i) -> p c j i", i=4),
+                out=grouped[:].rearrange("p (c i) j -> p c j i", i=4),
+                in_=wa_raw[n][:].rearrange("p j (c i) -> p c j i", i=4),
             )
-            grouped[key] = wide
+            return grouped
 
-        def quantize(key):
-            codes = keep.tile([P, HALF], U32, name="wa_codes%d%d" % key, align_bytes=64)
-            plane = keep.tile([P, HALF], U8, name="wa_plane%d%d" % key, align_bytes=64)
+        def quantize(n, grouped):
+            g, lo, hi = pieces[n]
             nc.vector.quantize_mx(
-                out=codes[:].bitcast(FP8X4), scales=plane[:], in_=grouped[key][:].rearrange("p c j -> p (c j)")
+                out=wa_codes[:, g, lo:hi].bitcast(FP8X4),
+                scales=wa_s[:, g, lo:hi],
+                in_=grouped[:].rearrange("p c j -> p (c j)"),
             )
-            wa_codes[key], wa_planes[key] = codes, plane
 
-        cast(pieces[0])
+        last_grouped = cast(0)
         for n in range(1, len(pieces)):
-            cast(pieces[n])
-            quantize(pieces[n - 1])
-        quantize(pieces[-1])
-
-        def wa_cols(i):
-            h, c = divmod(i, 2)
-            return lambda g: (
-                wa_codes[g, h][:, P * c : P * (c + 1)].bitcast(FP8X4),
-                wa_planes[g, h][:, P * c : P * (c + 1)],
-            )
+            previous, last_grouped = last_grouped, cast(n)
+            quantize(n - 1, previous)
 
         def softplus(name, sig, pre):
             log_sig = work("ln_" + name)
@@ -180,10 +171,12 @@ def tile_mix_precision_weighted_sums_kernel(
         pa, pb, total, a, b = [], [], [], [], []
         for i in range(TILES):
             pa.append(softplus("pa%d" % i, su[i], u[i]))
+            if i == 0:
+                quantize(len(pieces) - 1, last_grouped)
             pb.append(softplus("pb%d" % i, sv[i], v[i]))
             total.append(work("total%d" % i))
             nc.gpsimd.tensor_tensor(out=total[i][:], in0=pa[i][:], in1=pb[i][:], op=ALU.add)
-            a.append(product("first%d" % i, wa_cols(i), xt_pass))
+            a.append(product("first%d" % i, fp8_cols(wa_codes, wa_s, i), xt_pass))
             b.append(product("second%d" % i, fp8_cols(wq, wq_s, i), xq_pass))
 
         root = [work("root%d" % i) for i in range(TILES)]

from contextlib import ExitStack

import concourse.mybir as mybir

K, T, N = 1024, 512, 512
FLOPS = 4 * 2 * K * T * N

F32 = mybir.dt.float32
BF16 = mybir.dt.bfloat16
I32 = mybir.dt.int32
U32 = mybir.dt.uint32
U8 = mybir.dt.uint8
FP8X4 = mybir.dt.float8_e4m3fn_x4
FP4X4 = mybir.dt.float4_e2m1fn_x4
ACT = mybir.ActivationFunctionType
ALU = mybir.AluOpType

P = 128
PACK = 4
PASSES = K // (P * PACK)
TILES = N // P
HALF = N // 2
TINY = 2.0**-46
WARM_NARROW = 10
WARM_WIDE = 4


def tile_mix_precision_weighted_sums_kernel(
    tc, xt_words, xt_scales, wa, xq_words, xq_scales, wq_words, wq_scales, vb_words, vb_scales, va_words, va_scales, out
):
    nc = tc.nc
    with ExitStack() as ctx:
        keep = ctx.enter_context(tc.tile_pool(name="keep", bufs=1))
        psum = ctx.enter_context(tc.psum_pool(name="psum", bufs=1))
        ctx.enter_context(tc.manual_schedule())

        def plane_tile(name):
            plane = keep.tile([P, PASSES, 512], U8, name=name, align_bytes=64)
            nc.vector.memset(plane[:].bitcast(I32), 0)
            return plane

        def load_scales(queue, plane, scales, quadrants):
            for q in quadrants:
                queue.dma_start(
                    out=plane[32 * q : 32 * q + 4, :, :].bitcast(I32),
                    in_=scales[:, 4 * q : 4 * q + 4, :].rearrange("g r n -> r g n").bitcast(I32),
                )

        def load_fp8(name, words):
            codes = keep.tile([P, PASSES, 512], U32, name=name, align_bytes=64)
            nc.sync.dma_start(out=codes[:].bitcast(I32), in_=words.rearrange("g p n t -> p g (n t)").bitcast(I32))
            return codes

        def load_fp4(name, words):
            codes = keep.tile([P, PASSES, 1024], U8, name=name, align_bytes=64)
            nc.sync.dma_start(out=codes[:].bitcast(I32), in_=words.rearrange("g p b -> p g b").bitcast(I32))
            return codes

        xq_s = plane_tile("xq_s")
        va_s = plane_tile("va_s")
        ones = keep.tile([P, PACK * P], BF16, name="ones", align_bytes=64)
        nc.vector.memset(ones[:], 1.0)
        vb_s = plane_tile("vb_s")
        ones_codes = keep.tile([P, P], U32, name="ones_codes", align_bytes=64)
        ones_plane = keep.tile([P, P], U8, name="ones_plane", align_bytes=64)
        nc.vector.quantize_mx(out=ones_codes[:].bitcast(FP8X4), scales=ones_plane[:], in_=ones[:])
        xt_s = plane_tile("xt_s")
        wq_s = plane_tile("wq_s")
        warm = keep.tile([P, 8], F32, name="warm")
        nc.vector.memset(warm[:], 0.0)

        warm_out = keep.tile([P, 8], F32, name="warm_out")
        nc.scalar.activation(out=warm_out[:], in_=warm[:], func=ACT.Sigmoid)
        xq = load_fp4("xq", xq_words)
        load_scales(nc.sync, xq_s, xq_scales, range(4))
        load_scales(nc.sync, va_s, va_scales, range(2))
        va = load_fp8("va", va_words)
        load_scales(nc.sync, va_s, va_scales, range(2, 4))
        load_scales(nc.gpsimd, vb_s, vb_scales, range(2, 4))
        load_scales(nc.gpsimd, wq_s, wq_scales, range(4))
        vb = load_fp4("vb", vb_words)
        xt = load_fp8("xt", xt_words)
        load_scales(nc.sync, xt_s, xt_scales, range(4))
        load_scales(nc.sync, vb_s, vb_scales, range(2))

        def load_wa(g, cols):
            raw = keep.tile([P, PACK, cols.stop - cols.start], F32, name="wa_raw%d_%d" % (g, cols.start))
            nc.sync.dma_start(out=raw[:], in_=wa[512 * g : 512 * (g + 1), cols].rearrange("(p j) n -> p j n", j=PACK))
            return raw

        pieces = [(0, 0, 256), (0, 256, 512), (1, 0, 256), (1, 256, 384), (1, 384, 512)]
        wa_raw = [load_wa(g, slice(lo, hi)) for g, lo, hi in pieces]
        wq = load_fp8("wq", wq_words)

        def product(bank, lhs, rhs):
            acc = psum.tile([P, T], F32, name=bank, tag=bank)
            for g in range(PASSES):
                lc, ls = lhs(g)
                rc, rs = rhs(g)
                nc.tensor.matmul_mx(
                    out=acc[:], lhsT=lc, lhsT_scale=ls, rhs=rc, rhs_scale=rs, start=(g == 0), stop=(g == PASSES - 1)
                )
            return acc

        def xq_pass(g):
            return xq[:, g, :].bitcast(FP4X4), xq_s[:, g, :]

        def xt_pass(g):
            return xt[:, g, :].bitcast(FP8X4), xt_s[:, g, :]

        def fp8_cols(codes, plane, i):
            return lambda g: (codes[:, g, P * i : P * (i + 1)].bitcast(FP8X4), plane[:, g, P * i : P * (i + 1)])

        def fp4_cols(codes, plane, i):
            return lambda g: (codes[:, g, 2 * P * i : 2 * P * (i + 1)].bitcast(FP4X4), plane[:, g, P * i : P * (i + 1)])

        def work(name):
            return keep.tile([P, T], F32, name=name)

        idle = psum.tile([P, T], F32, name="idle", tag="second3")
        ones_mx = dict(lhsT=ones_codes[:].bitcast(FP8X4), lhsT_scale=ones_plane[:], start=True, stop=True)
        for n in range(WARM_NARROW):
            nc.tensor.matmul_mx(out=idle[:, 0:P], rhs=ones_codes[:].bitcast(FP8X4), rhs_scale=ones_plane[:], **ones_mx)
        for n in range(WARM_WIDE):
            nc.tensor.matmul_mx(out=idle[:], rhs=xq_pass(0)[0], rhs_scale=xq_pass(0)[1], **ones_mx)

        u = [product("first%d" % i, fp8_cols(va, va_s, i), xq_pass) for i in range(TILES)]
        v = [product("second%d" % i, fp4_cols(vb, vb_s, i), xt_pass) for i in range(TILES)]

        su = [work("su%d" % i) for i in range(TILES)]
        sv = [work("sv%d" % i) for i in range(TILES)]
        for i in range(TILES):
            nc.scalar.activation(out=su[i][:], in_=u[i][:], func=ACT.Sigmoid, scale=-1.0)
        for i in range(TILES):
            nc.scalar.activation(out=sv[i][:], in_=v[i][:], func=ACT.Sigmoid, scale=-1.0)

        wa_codes = keep.tile([P, PASSES, N], U32, name="wa_codes", align_bytes=64)
        wa_s = keep.tile([P, PASSES, N], U8, name="wa_s", align_bytes=64)

        def cast(n):
            g, lo, hi = pieces[n]
            grouped = keep.tile([P, hi - lo, PACK], BF16, name="grouped%d" % n, align_bytes=64)
            nc.vector.tensor_copy(
                out=grouped[:].rearrange("p (c i) j -> p c j i", i=4),
                in_=wa_raw[n][:].rearrange("p j (c i) -> p c j i", i=4),
            )
            return grouped

        def quantize(n, grouped):
            g, lo, hi = pieces[n]
            nc.vector.quantize_mx(
                out=wa_codes[:, g, lo:hi].bitcast(FP8X4),
                scales=wa_s[:, g, lo:hi],
                in_=grouped[:].rearrange("p c j -> p (c j)"),
            )

        last_grouped = cast(0)
        for n in range(1, len(pieces)):
            previous, last_grouped = last_grouped, cast(n)
            quantize(n - 1, previous)

        def softplus(name, sig, pre):
            log_sig = work("ln_" + name)
            nc.scalar.activation(out=log_sig[:], in_=sig[:], func=ACT.Ln, bias=TINY)
            result = work(name)
            nc.vector.scalar_tensor_tensor(
                out=result[:], in0=log_sig[:], scalar=-1.0, in1=pre[:], op0=ALU.mult, op1=ALU.max
            )
            return result

        pa, pb, total, a, b = [], [], [], [], []
        for i in range(TILES):
            pa.append(softplus("pa%d" % i, su[i], u[i]))
            if i == 0:
                quantize(len(pieces) - 1, last_grouped)
            pb.append(softplus("pb%d" % i, sv[i], v[i]))
            total.append(work("total%d" % i))
            nc.gpsimd.tensor_tensor(out=total[i][:], in0=pa[i][:], in1=pb[i][:], op=ALU.add)
            a.append(product("first%d" % i, fp8_cols(wa_codes, wa_s, i), xt_pass))
            b.append(product("second%d" % i, fp8_cols(wq, wq_s, i), xq_pass))

        root = [work("root%d" % i) for i in range(TILES)]
        inverse = [work("inverse%d" % i) for i in range(TILES)]
        for i in range(TILES):
            nc.scalar.activation(out=root[i][:], in_=total[i][:], func=ACT.Abs_reciprocal_sqrt, bias=0.1)
            nc.scalar.activation(out=inverse[i][:], in_=root[i][:], func=ACT.Square)

        na = [work("na%d" % i) for i in range(TILES)]
        nb = [work("nb%d" % i) for i in range(TILES)]
        num = [work("num%d" % i) for i in range(TILES)]
        for i in range(TILES):
            nc.vector.tensor_tensor(out=na[i][:], in0=a[i][:], in1=pa[i][:], op=ALU.mult)
            nc.vector.tensor_tensor(out=nb[i][:], in0=b[i][:], in1=pb[i][:], op=ALU.mult)
            if i < 2:
                nc.gpsimd.tensor_tensor(out=num[i][:], in0=na[i][:], in1=nb[i][:], op=ALU.add)

        def finish(i, parts=1):
            width = T // parts
            for c in range(0, T, width):
                y = keep.tile([P, width], F32, name="y%d_%d" % (i, c))
                cols = slice(c, c + width)
                nc.vector.tensor_tensor(out=y[:], in0=num[i][:, cols], in1=inverse[i][:, cols], op=ALU.mult)
                nc.sync.dma_start(out=out[P * i : P * (i + 1), cols], in_=y[:])

        finish(0)
        nc.vector.tensor_tensor(out=num[2][:], in0=na[2][:], in1=nb[2][:], op=ALU.add)
        finish(1)
        nc.vector.tensor_tensor(out=num[3][:], in0=na[3][:], in1=nb[3][:], op=ALU.add)
        finish(2)
        finish(3, 2)
